import numpy as np
import ml_dtypes


def mxq(x, axis, fmt="e4m3"):
    dtype, down = {"e4m3": (ml_dtypes.float8_e4m3fn, 7), "e5m2": (ml_dtypes.float8_e5m2, 14)}[fmt]
    v = np.moveaxis(np.asarray(x, np.float32).astype(ml_dtypes.bfloat16).astype(np.float64), axis, -1)
    blocks = v.reshape(v.shape[:-1] + (-1, 32))
    amax = np.abs(blocks).max(-1, keepdims=True)
    byte = np.maximum(np.where(amax > 0, np.frexp(amax)[1] - 1 + 127, 0) - down, 1)
    scale = np.exp2(byte - 127.0)
    codes = (blocks / scale).astype(np.float32).astype(dtype).astype(np.float64)
    return np.moveaxis((codes * scale).reshape(v.shape), -1, axis)


WIDE = False


def mx_kscale(k):
    if not WIDE:
        return np.ones(k)
    levels = np.array([10, -10, 5, -5, 0])
    if k % 512:
        return np.exp2(np.random.permutation(np.resize(levels, k // 32))).repeat(32)
    a = np.empty((k // 512, 16))
    for p in range(k // 512):
        a[p, :8] = np.random.permutation(np.resize(levels, 8))
        for g in range(8):
            far = levels[np.abs(levels - a[p, g]) >= 10]
            a[p, g + 8] = far[np.random.randint(len(far))]
    return np.exp2(a.ravel()).repeat(32)


BF16 = ml_dtypes.bfloat16


def bf(x):
    return np.asarray(x, np.float32).astype(BF16)


def f64(x):
    return np.asarray(x).astype(np.float64)


E2M1 = np.array([0.0, 0.5, 1.0, 1.5, 2.0, 3.0, 4.0, 6.0, -0.0, -0.5, -1.0, -1.5, -2.0, -3.0, -4.0, -6.0])


def pack_weight(w, fmt):
    k, n = w.shape
    w = f64(bf(w)).reshape(k // 32, 32, n)
    amax = np.abs(w).max(1)
    if fmt == "e4m3":
        byte = np.frexp(amax)[1] - 1 + 127 - 7
    else:
        mant, ex = np.frexp(amax / 6.0)
        byte = np.where(mant > 0.5, ex, ex - 1) + 127
    byte = np.clip(np.where(amax > 0, byte, 1), 1, 254)
    scaled = (w * np.exp2(127.0 - byte)[:, None, :]).reshape(k, n).astype(np.float32)
    by_word = np.ascontiguousarray(scaled.reshape(k // 512, 128, 4, n).transpose(0, 1, 3, 2))
    if fmt == "e4m3":
        words = by_word.astype(ml_dtypes.float8_e4m3fn).view(np.uint8)
    else:
        c = by_word.astype(ml_dtypes.float4_e2m1fn).view(np.uint8) & 0xF
        words = c[..., 0::2] | (c[..., 1::2] << 4)
    return np.ascontiguousarray(words), np.ascontiguousarray(byte.astype(np.uint8).reshape(k // 512, 16, n))


def unpack_weight(words, scales, fmt):
    g, p, n, _ = words.shape
    if fmt == "e4m3":
        vals = np.ascontiguousarray(words).view(ml_dtypes.float8_e4m3fn).astype(np.float64)
    else:
        nib = np.empty((g, p, n, 4), np.uint8)
        nib[..., 0::2] = words & 0xF
        nib[..., 1::2] = words >> 4
        vals = E2M1[nib]
    vals = vals * np.repeat(np.exp2(scales.astype(np.float64) - 127.0), 8, axis=1)[..., None]
    return vals.transpose(0, 1, 3, 2).reshape(g * 512, n)
def pack4(w):
    words, scales = pack_weight(w, "e2m1")
    return words.reshape(words.shape[0], 128, -1), scales


def unpack4(words, scales):
    return unpack_weight(words.reshape(words.shape[0], 128, -1, 2), scales, "e2m1")


E4M3FN = np.array([(-1.0 if i & 128 else 1.0) * ((1.0 + (i & 7) / 8.0) * 2.0 ** (((i >> 3) & 15) - 7) if i & 120 else (i & 7) * 2.0 ** -9) for i in range(256)])


def e4m3fn_bytes(y):
    return np.clip(np.asarray(y, np.float64), -448.0, 448.0).astype(np.float32).astype(ml_dtypes.float8_e4m3fn).view(np.uint8)


def e4m3fn_values(b):
    return E4M3FN[b]


N, E, D, M = 1024, 1024, 1536, 1024


def sinh_(t):
    return (np.exp(t) - np.exp(-t)) / 2.0


def cosh_(t):
    return (np.exp(t) + np.exp(-t)) / 2.0


def asinh_(u):
    mag = np.log(np.abs(u) + np.sqrt(u * u + 1.0))
    return np.where(u >= 0.0, mag, -mag)


def draw0():
    s, t = mx_kscale(E), mx_kscale(D)
    radius = np.random.uniform(0.5, 2.0, (N, 1))
    x = bf(np.random.standard_normal((N, E)) * radius * s)
    w_words, w_scales = pack4(np.random.standard_normal((E, D)) / np.sqrt(E) / s[:, None])
    gain = bf((1.0 + 0.1 * np.random.standard_normal(D)) * t)
    z_words, z_scales = pack4((np.random.standard_normal((M, D)) / np.sqrt(D) / t).T)
    return {"x": x,
            "w_words": w_words,
            "w_scales": w_scales,
            "gain": gain,
            "z_words": z_words,
            "z_scales": z_scales,
            "q": bf(0.5 * np.random.standard_normal(M)),
            "zeta": bf(1.0 + 0.1 * np.random.standard_normal(M))}


def core(x, w_words, w_scales, gain, z_words, z_scales, q, zeta):
    v = mxq(f64(x), 1, "e4m3") @ unpack4(w_words, w_scales)
    r = np.sqrt(np.mean(v * v, axis=-1) + 1e-6)
    vg = v * f64(gain)[None, :]
    m = mxq(vg, 1, "e4m3") @ unpack4(z_words, z_scales)
    sr = sinh_(r) / r
    h = cosh_(r)
    cq = cosh_(f64(q))
    sq = sinh_(f64(q))
    u = sr[:, None] * m * cq[None, :] - h[:, None] * sq[None, :]
    return 4.0 * f64(zeta)[None, :] * asinh_(u)


def setup_inputs():
    drawn = draw0()
    full = np.asarray(drawn['x']).astype(np.float64)
    scale = (np.abs(full).reshape(8, 128, 8, 128).max(axis=(1, 3)) / 448.0).astype(np.float32)
    given = {}
    for key, value in drawn.items():
        if key == 'x':
            given['x_bytes'] = e4m3fn_bytes(full / np.repeat(np.repeat(scale.astype(np.float64), 128, axis=0), 128, axis=1))
            given['x_scale'] = scale
        else:
            given[key] = value
    return given


def reference(x_bytes, x_scale, w_words, w_scales, gain, z_words, z_scales, q, zeta):
    return core(e4m3fn_values(x_bytes) * np.repeat(np.repeat(x_scale.astype(np.float64), 128, axis=0), 128, axis=1), w_words, w_scales, gain, z_words, z_scales, q, zeta)

@@ -1,0 +1,359 @@
+from contextlib import ExitStack
+
+import concourse.mybir as mybir
+from concourse.masks import make_identity
+
+N, E, D, M = 1024, 1024, 1536, 1024
+FLOPS = 2 * N * E * D + 2 * N * D * M
+
+F32 = mybir.dt.float32
+BF16 = mybir.dt.bfloat16
+I32 = mybir.dt.int32
+U32 = mybir.dt.uint32
+U8 = mybir.dt.uint8
+FP8 = mybir.dt.float8_e4m3fn
+FP8X4 = mybir.dt.float8_e4m3fn_x4
+FP4X4 = mybir.dt.float4_e2m1fn_x4
+ALU = mybir.AluOpType
+ACT = mybir.ActivationFunctionType
+
+P = 128
+BANK = 512
+TILES = N // P
+GE = E // 512
+GD = D // 512
+HM = M // BANK
+BATCH = 4
+LOG2E = 1.4426950408889634
+
+
+def tile_rmssinhcoshasinhlogits_kernel(tc, x_bytes, x_scale, w_words, w_scales, gain, z_words, z_scales, q, zeta, out):
+    nc = tc.nc
+    with ExitStack() as ctx:
+        keep = ctx.enter_context(tc.tile_pool(name="keep", bufs=1))
+        ring = ctx.enter_context(tc.tile_pool(name="ring", bufs=3))
+        psum = ctx.enter_context(tc.psum_pool(name="psum", bufs=1))
+        ctx.enter_context(tc.manual_schedule())
+
+        def bank(b, shape, dtype, name):
+            return psum.tile(shape, dtype, name=name, tag="bank%d" % b)
+
+        x_in = [keep.tile([P, E], U8, name="x_in%d" % i) for i in range(TILES)]
+        xsc = keep.tile([P, TILES * 8], F32, name="xsc")
+        w_sb = [keep.tile([P, GE, 1024], U8, name="w_sb%d" % h, align_bytes=64) for h in range(GD)]
+        w_sc = keep.tile([P, GE, D], U8, name="w_sc", align_bytes=64)
+        z_sb = keep.tile([P, GD, 2 * M], U8, name="z_sb", align_bytes=64)
+        z_sc = keep.tile([P, GD, M], U8, name="z_sc", align_bytes=64)
+        row_g = keep.tile([P, D], BF16, name="row_g")
+        row_q = keep.tile([P, M], BF16, name="row_q")
+        row_z = keep.tile([P, M], BF16, name="row_z")
+        ident = keep.tile([P, P], F32, name="ident")
+        ones1 = keep.tile([P, P], BF16, name="ones1")
+        ones8 = keep.tile([P, P], BF16, name="ones8")
+        onesf = keep.tile([P, P], F32, name="onesf")
+        c_two = keep.tile([P, BATCH], F32, name="c_two")
+        c_half = keep.tile([P, BATCH], F32, name="c_half")
+        c_neg = keep.tile([P, BATCH], F32, name="c_neg")
+        gain_t = keep.tile([P, D], BF16, name="gain_t")
+        ep = keep.tile([P, M], F32, name="ep")
+        em = keep.tile([P, M], F32, name="em")
+        cq = keep.tile([P, M], F32, name="cq")
+        sq = keep.tile([P, M], F32, name="sq")
+        vcodes = [keep.tile([P, GD * P], U32, name="vcodes%d" % i, align_bytes=64) for i in range(TILES)]
+        vscales = [keep.tile([P, GD * P], U8, name="vscales%d" % i, align_bytes=64) for i in range(TILES)]
+        ssq = [keep.tile([P, BATCH, GD], F32, name="ssq%d" % b) for b in range(TILES // BATCH)]
+        hfac = [keep.tile([P, BATCH], F32, name="hfac%d" % b) for b in range(TILES // BATCH)]
+        tau = [keep.tile([P, BATCH], F32, name="tau%d" % b) for b in range(TILES // BATCH)]
+        wsum = [keep.tile([P, M], F32, name="wsum%d" % i) for i in range(TILES)]
+        gsign = [keep.tile([P, M], BF16, name="gsign%d" % i) for i in range(TILES)]
+
+        nc.vector.memset(row_g[:].bitcast(I32), 0)
+        nc.vector.memset(row_q[:].bitcast(I32), 0)
+        nc.vector.memset(w_sc[:].bitcast(I32), 0)
+        nc.gpsimd.memset(ones1[:], 0.0)
+        nc.gpsimd.memset(ones1[0:1, :], 1.0)
+        make_identity(nc, ident[:])
+        nc.gpsimd.memset(row_z[:].bitcast(I32), 0)
+        nc.gpsimd.memset(z_sc[:].bitcast(I32), 0)
+        nc.gpsimd.memset(ones8[:], 0.0)
+        nc.gpsimd.memset(ones8[0:1, :], 8.0)
+        nc.gpsimd.memset(onesf[:], 0.0)
+        nc.gpsimd.memset(onesf[0:1, :], 1.0)
+        nc.gpsimd.memset(c_two[:], 2.0)
+        nc.gpsimd.memset(c_half[:], 0.5)
+        nc.gpsimd.memset(c_neg[:], -1.0)
+
+        def load_x(i):
+            nc.sync.dma_start(out=x_in[i][:], in_=x_bytes[i * P:(i + 1) * P, :])
+
+        def load_w(h):
+            src = w_words.rearrange("g p n -> p g n")[:, :, 1024 * h:1024 * (h + 1)]
+            nc.sync.dma_start(out=w_sb[h][:].bitcast(I32), in_=src.bitcast(I32))
+
+        nc.scalar.dma_start(out=xsc[:], in_=x_scale.rearrange("i j -> (i j)").partition_broadcast(P))
+        load_x(0)
+        nc.sync.dma_start(out=row_g[0:1, :], in_=gain.rearrange("(o n) -> o n", o=1))
+        nc.sync.dma_start(out=row_q[0:1, :], in_=q.rearrange("(o n) -> o n", o=1))
+        load_x(1)
+        for r in range(4):
+            nc.sync.dma_start(out=w_sc[32 * r:32 * r + 4, :, :].bitcast(I32), in_=w_scales[:, 4 * r:4 * r + 4, :].rearrange("g r n -> r g n").bitcast(I32))
+        load_w(0)
+        load_x(2)
+        load_w(1)
+        load_w(2)
+        for i in range(3, TILES):
+            load_x(i)
+        nc.sync.dma_start(out=row_z[0:1, :], in_=zeta.rearrange("(o n) -> o n", o=1))
+        for g in range(GD):
+            nc.sync.dma_start(out=z_sb[:, g, :].bitcast(I32), in_=z_words[g].bitcast(I32))
+        for r in range(4):
+            nc.sync.dma_start(out=z_sc[32 * r:32 * r + 4, :, :].bitcast(I32), in_=z_scales[:, 4 * r:4 * r + 4, :].rearrange("g r n -> r g n").bitcast(I32))
+
+        xb, xps, xg, xcodes, xscales = {}, {}, {}, {}, {}
+        vps, vg, vtps, vt = {}, {}, {}, {}
+        flips = []
+
+        def next_flip_bank(last):
+            b = 4 + len(flips) % (last - 3)
+            flips.append(b)
+            return b
+
+        def widen_v(i):
+            xb[i] = ring.tile([P, E], BF16, name="xb", align_bytes=64, bufs=4)
+            for j in range(8):
+                c = slice(P * j, P * (j + 1))
+                nc.vector.tensor_scalar(out=xb[i][:, c], in0=x_in[i][:, c].bitcast(FP8), scalar1=xsc[:, 8 * i + j:8 * i + j + 1], scalar2=None, op0=ALU.mult)
+
+        def flip_x(i):
+            xps[i] = bank(next_flip_bank(7), [P, GE, 2, P], F32, "xps")
+            words = xb[i][:].bitcast(F32)
+            for g in range(GE):
+                for u in range(2):
+                    nc.tensor.transpose(xps[i][:, g, u, :], words[:, 256 * g + u:256 * (g + 1):2], ident[:])
+
+        def evac_x(i, eng):
+            xg[i] = ring.tile([P, GE, P, 4], BF16, name="xg", align_bytes=64)
+            dst = xg[i][:].rearrange("p g n t -> p (g n t)").bitcast(F32).rearrange("p (g n u) -> p g n u", g=GE, u=2)
+            src = xps[i][:].rearrange("p g u n -> p g n u")
+            if eng == "v":
+                nc.vector.tensor_copy(out=dst, in_=src)
+            else:
+                nc.scalar.copy(out=dst, in_=src)
+
+        def quant_x(i):
+            xcodes[i] = ring.tile([P, GE * P], U32, name="xcodes", align_bytes=64)
+            xscales[i] = ring.tile([P, GE * P], U8, name="xscales", align_bytes=64)
+            nc.vector.quantize_mx(out=xcodes[i][:].bitcast(FP8X4), scales=xscales[i][:], in_=xg[i][:].rearrange("p g n t -> p (g n t)"))
+
+        def mm1(i):
+            for h in range(GD):
+                acc = bank((GD * i + h) % 4, [P, BANK], F32, "vps")
+                vps[i, h] = acc
+                for g in range(GE):
+                    nc.tensor.matmul_mx(out=acc[:], lhsT=xcodes[i][:, P * g:P * (g + 1)].bitcast(FP8X4), lhsT_scale=xscales[i][:, P * g:P * (g + 1)],
+                                        rhs=w_sb[h][:, g, :].bitcast(FP4X4), rhs_scale=w_sc[:, g, BANK * h:BANK * (h + 1)], start=(g == 0), stop=(g == GE - 1))
+
+        def gain_v(i, h):
+            if h == 0:
+                vg[i] = ring.tile([P, D], BF16, name="vg", align_bytes=64)
+            c = slice(BANK * h, BANK * (h + 1))
+            nc.vector.tensor_tensor(out=vg[i][:, c].rearrange("n (u p e) -> n u p e", u=2, e=2), in0=vps[i, h][:].rearrange("n (p u e) -> n u p e", u=2, e=2),
+                                    in1=gain_t[:, c].rearrange("n (u p e) -> n u p e", u=2, e=2), op=ALU.mult)
+
+        def square_s(i, h):
+            junk = ring.tile([P, BANK], BF16, name="junk", bufs=2)
+            nc.scalar.activation(out=junk[:], in_=vps[i, h][:], func=ACT.Square, accum_out=ssq[i // BATCH][:, i % BATCH, h:h + 1])
+
+        def flip_v(i):
+            words = vg[i][:].bitcast(F32)
+            ba, bb = (4, 5) if i >= 4 else (next_flip_bank(7), next_flip_bank(7))
+            a = bank(ba, [P, 2, 2, P], F32, "vta")
+            b = bank(bb, [P, 2, P], F32, "vtb")
+            vtps[i] = (a, b)
+            for g in range(2):
+                for u in range(2):
+                    nc.tensor.transpose(a[:, g, u, :], words[:, 256 * g + P * u:256 * g + P * (u + 1)], ident[:])
+            for u in range(2):
+                nc.tensor.transpose(b[:, u, :], words[:, 512 + P * u:512 + P * (u + 1)], ident[:])
+
+        def evac_v(i):
+            vt[i] = ring.tile([P, GD * P * 4], BF16, name="vt", align_bytes=64)
+            words = vt[i][:].bitcast(F32)
+            a, b = vtps[i]
+            nc.scalar.copy(out=words[:, 0:512].rearrange("p (g n u) -> p g n u", g=2, u=2), in_=a[:].rearrange("p g u n -> p g n u"))
+            nc.scalar.copy(out=words[:, 512:768].rearrange("p (n u) -> p n u", u=2), in_=b[:].rearrange("p u n -> p n u"))
+
+        def quant_v(i):
+            nc.vector.quantize_mx(out=vcodes[i][:, 0:256].bitcast(FP8X4), scales=vscales[i][:, 0:256], in_=vt[i][:, 0:1024])
+            nc.vector.quantize_mx(out=vcodes[i][:, 256:384].bitcast(FP8X4), scales=vscales[i][:, 256:384], in_=vt[i][:, 1024:1536])
+
+        def row_factors(b):
+            t = [ring.tile([P, BATCH], F32, name="rf%d" % k, bufs=1) for k in range(9)]
+            g = nc.gpsimd
+            s = ssq[b]
+            g.tensor_tensor(out=t[0][:], in0=s[:, :, 0], in1=s[:, :, 1], op=ALU.add)
+            g.tensor_tensor(out=t[1][:], in0=t[0][:], in1=s[:, :, 2], op=ALU.add)
+            g.tensor_scalar(out=t[2][:], in0=t[1][:], scalar1=1.0 / D, scalar2=1e-6, op0=ALU.mult, op1=ALU.add)
+            g.tensor_tensor(out=t[3][:], in0=t[2][:], in1=c_half[:], op=ALU.pow)
+            g.tensor_scalar(out=t[4][:], in0=t[3][:], scalar1=LOG2E, scalar2=0.0, op0=ALU.mult, op1=ALU.add)
+            g.tensor_tensor(out=t[5][:], in0=c_two[:], in1=t[4][:], op=ALU.pow)
+            g.tensor_tensor(out=t[6][:], in0=t[5][:], in1=c_neg[:], op=ALU.pow)
+            g.tensor_tensor(out=t[7][:], in0=t[5][:], in1=t[6][:], op=ALU.add)
+            g.tensor_tensor(out=t[8][:], in0=t[5][:], in1=t[6][:], op=ALU.subtract)
+            g.tensor_scalar(out=hfac[b][:], in0=t[7][:], scalar1=0.25, scalar2=0.0, op0=ALU.mult, op1=ALU.add)
+            g.tensor_tensor(out=t[4][:], in0=t[7][:], in1=t[3][:], op=ALU.mult)
+            g.tensor_tensor(out=t[5][:], in0=t[4][:], in1=c_neg[:], op=ALU.pow)
+            g.tensor_tensor(out=tau[b][:], in0=t[8][:], in1=t[5][:], op=ALU.mult)
+
+        gps, qps = {}, {}
+
+        def bcast_gain(h):
+            gps[h] = bank(h, [P, BANK], F32, "gps")
+            nc.tensor.matmul(gps[h][:], ones1[:], row_g[:, BANK * h:BANK * (h + 1)], start=True, stop=True)
+
+        def evac_gain(h, eng):
+            c = slice(BANK * h, BANK * (h + 1))
+            dst = gain_t[:, c].rearrange("n (u p e) -> n u p e", u=2, e=2)
+            src = gps[h][:].rearrange("n (p u e) -> n u p e", u=2, e=2)
+            if eng == "v":
+                nc.vector.tensor_copy(out=dst, in_=src)
+            else:
+                nc.scalar.copy(out=dst, in_=src)
+
+        def bcast_q(h, b):
+            qps[h] = bank(b, [P, BANK], F32, "qps")
+            nc.tensor.matmul(qps[h][:], ones1[:], row_q[:, BANK * h:BANK * (h + 1)], start=True, stop=True)
+
+        def exp_q(h):
+            c = slice(BANK * h, BANK * (h + 1))
+            nc.scalar.activation(out=ep[:, c], in_=qps[h][:], func=ACT.Exp)
+            nc.scalar.activation(out=em[:, c], in_=qps[h][:], func=ACT.Exp, scale=-1.0)
+
+        bcast_gain(0)
+        widen_v(0)
+        widen_v(1)
+        bcast_q(0, 6)
+        flip_x(0)
+        bcast_gain(1)
+        bcast_gain(2)
+        evac_gain(0, "v")
+        evac_x(0, "v")
+        flip_x(1)
+        exp_q(0)
+        evac_gain(1, "s")
+        bcast_q(1, 7)
+        widen_v(2)
+        quant_x(0)
+        evac_gain(2, "s")
+        evac_x(1, "s")
+        exp_q(1)
+        flip_x(2)
+        nc.gpsimd.tensor_tensor(out=cq[:], in0=ep[:], in1=em[:], op=ALU.add)
+        nc.gpsimd.tensor_tensor(out=sq[:], in0=ep[:], in1=em[:], op=ALU.subtract)
+
+        for i in range(TILES):
+            mm1(i)
+            if i + 2 < TILES:
+                evac_x(i + 2, "s")
+            if i >= 2:
+                evac_v(i - 2)
+            if i + 3 < TILES:
+                if i == 0:
+                    widen_v(3)
+                flip_x(i + 3)
+            if i >= 1:
+                flip_v(i - 1)
+            if i + 1 < TILES:
+                quant_x(i + 1)
+            if i >= 3:
+                quant_v(i - 3)
+            if i + 4 < TILES:
+                widen_v(i + 4)
+            for h in range(GD):
+                gain_v(i, h)
+                square_s(i, h)
+            if i % BATCH == BATCH - 1:
+                row_factors(i // BATCH)
+
+        mps, sqp, y_, q_, a_, sg_ = {}, {}, {}, {}, {}, {}
+
+        def mm2(j):
+            for h in range(HM):
+                acc = bank((2 * j + h) % 4, [P, BANK], F32, "mps")
+                mps[j, h] = acc
+                for g in range(GD):
+                    nc.tensor.matmul_mx(out=acc[:], lhsT=vcodes[j][:, P * g:P * (g + 1)].bitcast(FP8X4), lhsT_scale=vscales[j][:, P * g:P * (g + 1)],
+                                        rhs=z_sb[:, g, 1024 * h:1024 * (h + 1)].bitcast(FP4X4), rhs_scale=z_sc[:, g, BANK * h:BANK * (h + 1)],
+                                        start=(g == 0), stop=(g == GD - 1))
+
+        def logit_arg(j):
+            b, k = j // BATCH, j % BATCH
+            y1 = ring.tile([P, M], F32, name="y1", bufs=2)
+            y_[j] = ring.tile([P, M], F32, name="y")
+            for h in range(HM):
+                c = slice(BANK * h, BANK * (h + 1))
+                nc.vector.scalar_tensor_tensor(out=y1[:, c], in0=mps[j, h][:], scalar=tau[b][:, k:k + 1], in1=cq[:, c], op0=ALU.mult, op1=ALU.mult)
+            for h in range(HM):
+                c = slice(BANK * h, BANK * (h + 1))
+                nc.vector.tensor_tensor(out=y_[j][:, c], in0=y1[:, c], in1=sqp[h][:], op=ALU.subtract)
+
+        def square_abs(j):
+            b, k = j // BATCH, j % BATCH
+            q_[j] = ring.tile([P, M], F32, name="qq")
+            a_[j] = ring.tile([P, M], F32, name="aa")
+            nc.scalar.activation(out=q_[j][:], in_=y_[j][:], func=ACT.Square, scale=hfac[b][:, k:k + 1])
+            nc.scalar.activation(out=a_[j][:], in_=y_[j][:], func=ACT.Abs, scale=hfac[b][:, k:k + 1])
+
+        def root(j):
+            nc.scalar.activation(out=q_[j][:], in_=q_[j][:], func=ACT.Sqrt, bias=1.0)
+
+        def add_root(j):
+            nc.gpsimd.tensor_tensor(out=wsum[j][:], in0=a_[j][:], in1=q_[j][:], op=ALU.add)
+
+        def sign_half(j):
+            sg_[j] = ring.tile([P, M], BF16, name="sg")
+            nc.vector.tensor_scalar(out=sg_[j][:], in0=y_[j][:], scalar1=0.0, scalar2=0.5, op0=ALU.is_ge, op1=ALU.subtract)
+
+        def sign_gain(j):
+            nc.vector.tensor_tensor(out=gsign[j][:], in0=sg_[j][:], in1=zp[:], op=ALU.mult)
+
+        for h in range(HM):
+            sqp[h] = bank(6 + h, [P, BANK], F32, "sqp")
+            nc.tensor.matmul(sqp[h][:], onesf[:], sq[:, BANK * h:BANK * (h + 1)], start=True, stop=True)
+        mm2(0)
+        evac_v(TILES - 2)
+        flip_v(TILES - 1)
+        quant_v(TILES - 3)
+        logit_arg(0)
+        mm2(1)
+        square_abs(0)
+        evac_v(TILES - 1)
+        quant_v(TILES - 2)
+        zp = bank(5, [P, M], BF16, "zp")
+        for h in range(HM):
+            nc.tensor.matmul(zp[:, BANK * h:BANK * (h + 1)], ones8[:], row_z[:, BANK * h:BANK * (h + 1)], start=True, stop=True)
+        for j in range(TILES):
+            if j >= 1:
+                square_abs(j)
+            root(j)
+            add_root(j)
+            if j + 1 < TILES:
+                logit_arg(j + 1)
+            if j == 0:
+                quant_v(TILES - 1)
+            if j + 2 < TILES:
+                mm2(j + 2)
+            if j >= 1:
+                sign_gain(j - 1)
+            sign_half(j)
+        sign_gain(TILES - 1)
+
+        for j in range(TILES):
+            e = ring.tile([P, M], F32, name="e")
+            o = ring.tile([P, M], F32, name="o", bufs=4)
+            parts = 2 if j == TILES - 1 else 1
+            for k in range(parts):
+                c = slice(M // parts * k, M // parts * (k + 1))
+                nc.scalar.activation(out=e[:, c], in_=wsum[j][:, c], func=ACT.Ln)
+                nc.vector.tensor_tensor(out=o[:, c], in0=e[:, c], in1=gsign[j][:, c], op=ALU.mult)
+                nc.sync.dma_start(out=out[j * P:(j + 1) * P, c], in_=o[:, c])

@@ -23,7 +23,14 @@ TILES = N // P
 GE = E // 512
 GD = D // 512
 HM = M // BANK
-BATCH = 4
+BATCH = 2
+GSQ = ()
+WS = (1,)
+C2 = ()
+VEV = ()
+SSIGN = ()
+VADD = ()
+VEX = (0,)
 LOG2E = 1.4426950408889634
 
 
@@ -44,44 +51,51 @@ def tile_rmssinhcoshasinhlogits_kernel(tc, x_bytes, x_scale, w_words, w_scales, 
         w_sc = keep.tile([P, GE, D], U8, name="w_sc", align_bytes=64)
         z_sb = keep.tile([P, GD, 2 * M], U8, name="z_sb", align_bytes=64)
         z_sc = keep.tile([P, GD, M], U8, name="z_sc", align_bytes=64)
-        row_g = keep.tile([P, D], BF16, name="row_g")
-        row_q = keep.tile([P, M], BF16, name="row_q")
-        row_z = keep.tile([P, M], BF16, name="row_z")
-        ident = keep.tile([P, P], F32, name="ident")
-        ones1 = keep.tile([P, P], BF16, name="ones1")
-        ones8 = keep.tile([P, P], BF16, name="ones8")
-        onesf = keep.tile([P, P], F32, name="onesf")
-        c_two = keep.tile([P, BATCH], F32, name="c_two")
-        c_half = keep.tile([P, BATCH], F32, name="c_half")
-        c_neg = keep.tile([P, BATCH], F32, name="c_neg")
         gain_t = keep.tile([P, D], BF16, name="gain_t")
-        ep = keep.tile([P, M], F32, name="ep")
-        em = keep.tile([P, M], F32, name="em")
+        zeta_t = keep.tile([P, M], BF16, name="zeta_t")
+        ident = keep.tile([P, P], F32, name="ident")
+        onesf = keep.tile([P, P], F32, name="onesf")
+        onesb = keep.tile([P, P], BF16, name="onesb")
+        halfb = keep.tile([P, P], BF16, name="halfb")
+        c_two = keep.tile([P, 8], F32, name="c_two")
+        c_neg = keep.tile([P, 8], F32, name="c_neg")
+        warm = keep.tile([P, 1], F32, name="warm")
+        cqs = [keep.tile([P, 8], BF16 if k == 0 else F32, name="cqs%d" % k) for k in range(6)]
         cq = keep.tile([P, M], F32, name="cq")
         sq = keep.tile([P, M], F32, name="sq")
         vcodes = [keep.tile([P, GD * P], U32, name="vcodes%d" % i, align_bytes=64) for i in range(TILES)]
         vscales = [keep.tile([P, GD * P], U8, name="vscales%d" % i, align_bytes=64) for i in range(TILES)]
         ssq = [keep.tile([P, BATCH, GD], F32, name="ssq%d" % b) for b in range(TILES // BATCH)]
-        hfac = [keep.tile([P, BATCH], F32, name="hfac%d" % b) for b in range(TILES // BATCH)]
-        tau = [keep.tile([P, BATCH], F32, name="tau%d" % b) for b in range(TILES // BATCH)]
+        nh = [keep.tile([P, BATCH], F32, name="nh%d" % b) for b in range(TILES // BATCH)]
+        sig = [keep.tile([P, BATCH], F32, name="sig%d" % b) for b in range(TILES // BATCH)]
         wsum = [keep.tile([P, M], F32, name="wsum%d" % i) for i in range(TILES)]
         gsign = [keep.tile([P, M], BF16, name="gsign%d" % i) for i in range(TILES)]
 
-        nc.vector.memset(row_g[:].bitcast(I32), 0)
-        nc.vector.memset(row_q[:].bitcast(I32), 0)
-        nc.vector.memset(w_sc[:].bitcast(I32), 0)
-        nc.gpsimd.memset(ones1[:], 0.0)
-        nc.gpsimd.memset(ones1[0:1, :], 1.0)
-        make_identity(nc, ident[:])
-        nc.gpsimd.memset(row_z[:].bitcast(I32), 0)
-        nc.gpsimd.memset(z_sc[:].bitcast(I32), 0)
-        nc.gpsimd.memset(ones8[:], 0.0)
-        nc.gpsimd.memset(ones8[0:1, :], 8.0)
-        nc.gpsimd.memset(onesf[:], 0.0)
-        nc.gpsimd.memset(onesf[0:1, :], 1.0)
-        nc.gpsimd.memset(c_two[:], 2.0)
-        nc.gpsimd.memset(c_half[:], 0.5)
-        nc.gpsimd.memset(c_neg[:], -1.0)
+        def load_scale():
+            nc.scalar.dma_start(out=xsc[:], in_=x_scale.rearrange("i j -> (i j)").partition_broadcast(P))
+
+        def zero_wsc():
+            nc.vector.memset(w_sc[:].bitcast(I32), 0)
+
+        def zero_zsc():
+            nc.vector.memset(z_sc[:].bitcast(I32), 0)
+
+        def const_two():
+            nc.gpsimd.memset(c_two[:], 2.0)
+
+        def const_neg():
+            nc.gpsimd.memset(c_neg[:], -1.0)
+
+        def warm_up():
+            nc.scalar.activation(out=warm[:], in_=c_two[:, 0:1], func=ACT.Sqrt)
+
+        def identity():
+            make_identity(nc, ident[:])
+
+        def row_tile(k):
+            t, v = ((onesf, 1.0), (onesb, 1.0), (halfb, 0.5))[k]
+            nc.vector.memset(t[:], 0.0)
+            nc.vector.memset(t[0:1, :], v)
 
         def load_x(i):
             nc.sync.dma_start(out=x_in[i][:], in_=x_bytes[i * P:(i + 1) * P, :])
@@ -90,52 +104,69 @@ def tile_rmssinhcoshasinhlogits_kernel(tc, x_bytes, x_scale, w_words, w_scales, 
             src = w_words.rearrange("g p n -> p g n")[:, :, 1024 * h:1024 * (h + 1)]
             nc.sync.dma_start(out=w_sb[h][:].bitcast(I32), in_=src.bitcast(I32))
 
-        nc.scalar.dma_start(out=xsc[:], in_=x_scale.rearrange("i j -> (i j)").partition_broadcast(P))
-        load_x(0)
-        nc.sync.dma_start(out=row_g[0:1, :], in_=gain.rearrange("(o n) -> o n", o=1))
-        nc.sync.dma_start(out=row_q[0:1, :], in_=q.rearrange("(o n) -> o n", o=1))
-        load_x(1)
-        for r in range(4):
-            nc.sync.dma_start(out=w_sc[32 * r:32 * r + 4, :, :].bitcast(I32), in_=w_scales[:, 4 * r:4 * r + 4, :].rearrange("g r n -> r g n").bitcast(I32))
-        load_w(0)
-        load_x(2)
-        load_w(1)
-        load_w(2)
-        for i in range(3, TILES):
-            load_x(i)
-        nc.sync.dma_start(out=row_z[0:1, :], in_=zeta.rearrange("(o n) -> o n", o=1))
-        for g in range(GD):
+        def load_wsc():
+            for r in range(4):
+                nc.sync.dma_start(out=w_sc[32 * r:32 * r + 4, :, :].bitcast(I32), in_=w_scales[:, 4 * r:4 * r + 4, :].rearrange("g r n -> r g n").bitcast(I32))
+
+        def load_q():
+            nc.sync.dma_start(out=cqs[0][:], in_=q.rearrange("(p j) -> p j", j=8))
+
+        def load_gain():
+            nc.sync.dma_start(out=gain_t[:], in_=gain.partition_broadcast(P))
+
+        def load_zeta():
+            nc.sync.dma_start(out=zeta_t[:], in_=zeta.partition_broadcast(P))
+
+        def load_z(g):
             nc.sync.dma_start(out=z_sb[:, g, :].bitcast(I32), in_=z_words[g].bitcast(I32))
-        for r in range(4):
-            nc.sync.dma_start(out=z_sc[32 * r:32 * r + 4, :, :].bitcast(I32), in_=z_scales[:, 4 * r:4 * r + 4, :].rearrange("g r n -> r g n").bitcast(I32))
+
+        def load_zsc():
+            for r in range(4):
+                nc.sync.dma_start(out=z_sc[32 * r:32 * r + 4, :, :].bitcast(I32), in_=z_scales[:, 4 * r:4 * r + 4, :].rearrange("g r n -> r g n").bitcast(I32))
+
+        def column_factors():
+            g = nc.gpsimd
+            t = cqs
+            g.tensor_scalar(out=t[1][:], in0=t[0][:], scalar1=LOG2E, scalar2=0.0, op0=ALU.mult, op1=ALU.add)
+            g.tensor_tensor(out=t[2][:], in0=c_two[:], in1=t[1][:], op=ALU.pow)
+            g.tensor_tensor(out=t[3][:], in0=t[2][:], in1=c_neg[:], op=ALU.pow)
+            g.tensor_tensor(out=t[4][:], in0=t[2][:], in1=t[3][:], op=ALU.add)
+            g.tensor_tensor(out=t[5][:], in0=t[2][:], in1=t[3][:], op=ALU.subtract)
+
+        def park(k):
+            row = out[N - 8 + k:N - 7 + k, :]
+            nc.sync.dma_start(out=row.rearrange("o (p j) -> (o p) j", j=8), in_=cqs[k][:])
+
+        def fetch(k):
+            row = out[N - 8 + k:N - 7 + k, :]
+            nc.sync.dma_start(out=(cq if k == 4 else sq)[:], in_=row.rearrange("o c -> (o c)").partition_broadcast(P))
 
         xb, xps, xg, xcodes, xscales = {}, {}, {}, {}, {}
         vps, vg, vtps, vt = {}, {}, {}, {}
-        flips = []
+        XB = (4, 5, 6, 7, 4, 7, 6, 5)
+        VB = ((5, 6), (4, 5), (7, 4), (6, 7), (4, 5), (4, 5), (4, 5), (4, 5))
 
-        def next_flip_bank(last):
-            b = 4 + len(flips) % (last - 3)
-            flips.append(b)
-            return b
-
-        def widen_v(i):
+        def widen(i):
             xb[i] = ring.tile([P, E], BF16, name="xb", align_bytes=64, bufs=4)
             for j in range(8):
                 c = slice(P * j, P * (j + 1))
-                nc.vector.tensor_scalar(out=xb[i][:, c], in0=x_in[i][:, c].bitcast(FP8), scalar1=xsc[:, 8 * i + j:8 * i + j + 1], scalar2=None, op0=ALU.mult)
+                if i in WS:
+                    nc.scalar.activation(out=xb[i][:, c], in_=x_in[i][:, c].bitcast(FP8), func=ACT.Copy, scale=xsc[:, 8 * i + j:8 * i + j + 1])
+                else:
+                    nc.vector.tensor_scalar(out=xb[i][:, c], in0=x_in[i][:, c].bitcast(FP8), scalar1=xsc[:, 8 * i + j:8 * i + j + 1], scalar2=None, op0=ALU.mult)
 
         def flip_x(i):
-            xps[i] = bank(next_flip_bank(7), [P, GE, 2, P], F32, "xps")
+            xps[i] = bank(XB[i], [P, GE, 2, P], F32, "xps")
             words = xb[i][:].bitcast(F32)
             for g in range(GE):
                 for u in range(2):
                     nc.tensor.transpose(xps[i][:, g, u, :], words[:, 256 * g + u:256 * (g + 1):2], ident[:])
 
-        def evac_x(i, eng):
+        def evac_x(i):
             xg[i] = ring.tile([P, GE, P, 4], BF16, name="xg", align_bytes=64)
             dst = xg[i][:].rearrange("p g n t -> p (g n t)").bitcast(F32).rearrange("p (g n u) -> p g n u", g=GE, u=2)
             src = xps[i][:].rearrange("p g u n -> p g n u")
-            if eng == "v":
+            if i in VEX:
                 nc.vector.tensor_copy(out=dst, in_=src)
             else:
                 nc.scalar.copy(out=dst, in_=src)
@@ -145,215 +176,476 @@ def tile_rmssinhcoshasinhlogits_kernel(tc, x_bytes, x_scale, w_words, w_scales, 
             xscales[i] = ring.tile([P, GE * P], U8, name="xscales", align_bytes=64)
             nc.vector.quantize_mx(out=xcodes[i][:].bitcast(FP8X4), scales=xscales[i][:], in_=xg[i][:].rearrange("p g n t -> p (g n t)"))
 
-        def mm1(i):
-            for h in range(GD):
-                acc = bank((GD * i + h) % 4, [P, BANK], F32, "vps")
-                vps[i, h] = acc
-                for g in range(GE):
-                    nc.tensor.matmul_mx(out=acc[:], lhsT=xcodes[i][:, P * g:P * (g + 1)].bitcast(FP8X4), lhsT_scale=xscales[i][:, P * g:P * (g + 1)],
-                                        rhs=w_sb[h][:, g, :].bitcast(FP4X4), rhs_scale=w_sc[:, g, BANK * h:BANK * (h + 1)], start=(g == 0), stop=(g == GE - 1))
+        def mm1(i, h):
+            acc = bank((GD * i + h) % 4, [P, BANK], F32, "vps")
+            vps[i, h] = acc
+            for g in range(GE):
+                nc.tensor.matmul_mx(out=acc[:], lhsT=xcodes[i][:, P * g:P * (g + 1)].bitcast(FP8X4), lhsT_scale=xscales[i][:, P * g:P * (g + 1)],
+                                    rhs=w_sb[h][:, g, :].bitcast(FP4X4), rhs_scale=w_sc[:, g, BANK * h:BANK * (h + 1)], start=(g == 0), stop=(g == GE - 1))
 
         def gain_v(i, h):
             if h == 0:
                 vg[i] = ring.tile([P, D], BF16, name="vg", align_bytes=64)
             c = slice(BANK * h, BANK * (h + 1))
             nc.vector.tensor_tensor(out=vg[i][:, c].rearrange("n (u p e) -> n u p e", u=2, e=2), in0=vps[i, h][:].rearrange("n (p u e) -> n u p e", u=2, e=2),
-                                    in1=gain_t[:, c].rearrange("n (u p e) -> n u p e", u=2, e=2), op=ALU.mult)
+                                    in1=gain_t[:, c].rearrange("n (p u e) -> n u p e", u=2, e=2), op=ALU.mult)
 
         def square_s(i, h):
             junk = ring.tile([P, BANK], BF16, name="junk", bufs=2)
             nc.scalar.activation(out=junk[:], in_=vps[i, h][:], func=ACT.Square, accum_out=ssq[i // BATCH][:, i % BATCH, h:h + 1])
 
-        def flip_v(i):
+        def flip_v(i, k):
             words = vg[i][:].bitcast(F32)
-            ba, bb = (4, 5) if i >= 4 else (next_flip_bank(7), next_flip_bank(7))
-            a = bank(ba, [P, 2, 2, P], F32, "vta")
-            b = bank(bb, [P, 2, P], F32, "vtb")
-            vtps[i] = (a, b)
-            for g in range(2):
+            if k == 0:
+                a = bank(VB[i][0], [P, 2, 2, P], F32, "vta")
+                for g in range(2):
+                    for u in range(2):
+                        nc.tensor.transpose(a[:, g, u, :], words[:, 256 * g + P * u:256 * g + P * (u + 1)], ident[:])
+            else:
+                a = bank(VB[i][1], [P, 2, P], F32, "vtb")
                 for u in range(2):
-                    nc.tensor.transpose(a[:, g, u, :], words[:, 256 * g + P * u:256 * g + P * (u + 1)], ident[:])
-            for u in range(2):
-                nc.tensor.transpose(b[:, u, :], words[:, 512 + P * u:512 + P * (u + 1)], ident[:])
+                    nc.tensor.transpose(a[:, u, :], words[:, 512 + P * u:512 + P * (u + 1)], ident[:])
+            vtps[i, k] = a
 
-        def evac_v(i):
-            vt[i] = ring.tile([P, GD * P * 4], BF16, name="vt", align_bytes=64)
+        def evac_v(i, k):
+            if k == 0:
+                vt[i] = ring.tile([P, GD * P * 4], BF16, name="vt", align_bytes=64)
             words = vt[i][:].bitcast(F32)
-            a, b = vtps[i]
-            nc.scalar.copy(out=words[:, 0:512].rearrange("p (g n u) -> p g n u", g=2, u=2), in_=a[:].rearrange("p g u n -> p g n u"))
-            nc.scalar.copy(out=words[:, 512:768].rearrange("p (n u) -> p n u", u=2), in_=b[:].rearrange("p u n -> p n u"))
-
-        def quant_v(i):
-            nc.vector.quantize_mx(out=vcodes[i][:, 0:256].bitcast(FP8X4), scales=vscales[i][:, 0:256], in_=vt[i][:, 0:1024])
-            nc.vector.quantize_mx(out=vcodes[i][:, 256:384].bitcast(FP8X4), scales=vscales[i][:, 256:384], in_=vt[i][:, 1024:1536])
-
-        def row_factors(b):
-            t = [ring.tile([P, BATCH], F32, name="rf%d" % k, bufs=1) for k in range(9)]
-            g = nc.gpsimd
-            s = ssq[b]
-            g.tensor_tensor(out=t[0][:], in0=s[:, :, 0], in1=s[:, :, 1], op=ALU.add)
-            g.tensor_tensor(out=t[1][:], in0=t[0][:], in1=s[:, :, 2], op=ALU.add)
-            g.tensor_scalar(out=t[2][:], in0=t[1][:], scalar1=1.0 / D, scalar2=1e-6, op0=ALU.mult, op1=ALU.add)
-            g.tensor_tensor(out=t[3][:], in0=t[2][:], in1=c_half[:], op=ALU.pow)
-            g.tensor_scalar(out=t[4][:], in0=t[3][:], scalar1=LOG2E, scalar2=0.0, op0=ALU.mult, op1=ALU.add)
-            g.tensor_tensor(out=t[5][:], in0=c_two[:], in1=t[4][:], op=ALU.pow)
-            g.tensor_tensor(out=t[6][:], in0=t[5][:], in1=c_neg[:], op=ALU.pow)
-            g.tensor_tensor(out=t[7][:], in0=t[5][:], in1=t[6][:], op=ALU.add)
-            g.tensor_tensor(out=t[8][:], in0=t[5][:], in1=t[6][:], op=ALU.subtract)
-            g.tensor_scalar(out=hfac[b][:], in0=t[7][:], scalar1=0.25, scalar2=0.0, op0=ALU.mult, op1=ALU.add)
-            g.tensor_tensor(out=t[4][:], in0=t[7][:], in1=t[3][:], op=ALU.mult)
-            g.tensor_tensor(out=t[5][:], in0=t[4][:], in1=c_neg[:], op=ALU.pow)
-            g.tensor_tensor(out=tau[b][:], in0=t[8][:], in1=t[5][:], op=ALU.mult)
-
-        gps, qps = {}, {}
-
-        def bcast_gain(h):
-            gps[h] = bank(h, [P, BANK], F32, "gps")
-            nc.tensor.matmul(gps[h][:], ones1[:], row_g[:, BANK * h:BANK * (h + 1)], start=True, stop=True)
-
-        def evac_gain(h, eng):
-            c = slice(BANK * h, BANK * (h + 1))
-            dst = gain_t[:, c].rearrange("n (u p e) -> n u p e", u=2, e=2)
-            src = gps[h][:].rearrange("n (p u e) -> n u p e", u=2, e=2)
-            if eng == "v":
+            if k == 0:
+                dst = words[:, 0:512].rearrange("p (g n u) -> p g n u", g=2, u=2)
+                src = vtps[i, k][:].rearrange("p g u n -> p g n u")
+            else:
+                dst = words[:, 512:768].rearrange("p (n u) -> p n u", u=2)
+                src = vtps[i, k][:].rearrange("p u n -> p n u")
+            if (i, k) in VEV:
                 nc.vector.tensor_copy(out=dst, in_=src)
             else:
                 nc.scalar.copy(out=dst, in_=src)
 
-        def bcast_q(h, b):
-            qps[h] = bank(b, [P, BANK], F32, "qps")
-            nc.tensor.matmul(qps[h][:], ones1[:], row_q[:, BANK * h:BANK * (h + 1)], start=True, stop=True)
+        def quant_v(i, k):
+            c = slice(0, 256) if k == 0 else slice(256, 384)
+            nc.vector.quantize_mx(out=vcodes[i][:, c].bitcast(FP8X4), scales=vscales[i][:, c], in_=vt[i][:, 4 * c.start:4 * c.stop])
 
-        def exp_q(h):
+        rf = {}
+
+        def row_sum(b):
+            t = [keep.tile([P, BATCH], F32, name="rf%d_%d" % (b, k)) for k in range(9)]
+            rf[b] = t
+            g = nc.gpsimd
+            g.tensor_tensor(out=t[0][:], in0=ssq[b][:, :, 0], in1=ssq[b][:, :, 1], op=ALU.add)
+            g.tensor_tensor(out=t[1][:], in0=t[0][:], in1=ssq[b][:, :, 2], op=ALU.add)
+            g.tensor_scalar(out=t[2][:], in0=t[1][:], scalar1=16.0 / D, scalar2=16e-6, op0=ALU.mult, op1=ALU.add)
+
+        def row_root(b):
+            nc.scalar.activation(out=rf[b][3][:], in_=rf[b][2][:], func=ACT.Sqrt)
+
+        def row_factors(b):
+            t = rf[b]
+            g = nc.gpsimd
+            two, neg = c_two[:, 0:BATCH], c_neg[:, 0:BATCH]
+            g.tensor_scalar(out=t[4][:], in0=t[3][:], scalar1=LOG2E / 4, scalar2=0.0, op0=ALU.mult, op1=ALU.add)
+            g.tensor_tensor(out=t[5][:], in0=two, in1=t[4][:], op=ALU.pow)
+            g.tensor_tensor(out=t[6][:], in0=t[5][:], in1=neg, op=ALU.pow)
+            g.tensor_tensor(out=t[7][:], in0=t[3][:], in1=neg, op=ALU.pow)
+            g.tensor_tensor(out=t[8][:], in0=t[5][:], in1=t[6][:], op=ALU.subtract)
+            g.tensor_tensor(out=sig[b][:], in0=t[8][:], in1=t[7][:], op=ALU.mult)
+            g.tensor_tensor(out=t[0][:], in0=t[5][:], in1=t[6][:], op=ALU.add)
+            g.tensor_scalar(out=nh[b][:], in0=t[0][:], scalar1=-0.25, scalar2=0.0, op0=ALU.mult, op1=ALU.add)
+
+        mps, sqp, y_, y1_, q_, a_, sg_ = {}, {}, {}, {}, {}, {}, {}
+
+        def spread_sq(h):
+            sqp[h] = bank(6 + h, [P, BANK], F32, "sqp")
+            nc.tensor.matmul(sqp[h][:], onesf[:], sq[:, BANK * h:BANK * (h + 1)], start=True, stop=True)
+
+        def spread_zeta(k):
+            zp[k] = bank(5 - k, [P, M], BF16, "zp%d" % k)
+            for h in range(HM):
+                c = slice(BANK * h, BANK * (h + 1))
+                nc.tensor.matmul(zp[k][:, c], (halfb if k else onesb)[:], zeta_t[:, c], start=True, stop=True)
+
+        zp = {}
+
+        def mm2(j, h):
+            acc = bank(6 + h if j == 0 else (2 * j + h) % 4, [P, BANK], F32, "mps")
+            mps[j, h] = acc
+            for g in range(GD):
+                nc.tensor.matmul_mx(out=acc[:], lhsT=vcodes[j][:, P * g:P * (g + 1)].bitcast(FP8X4), lhsT_scale=vscales[j][:, P * g:P * (g + 1)],
+                                    rhs=z_sb[:, g, 1024 * h:1024 * (h + 1)].bitcast(FP4X4), rhs_scale=z_sc[:, g, BANK * h:BANK * (h + 1)],
+                                    start=(g == 0), stop=(g == GD - 1))
+
+        def logit_mul(j, h):
+            b, k = j // BATCH, j % BATCH
+            if h == 0:
+                y1_[j] = ring.tile([P, M], F32, name="y1", bufs=2)
+                y_[j] = ring.tile([P, M], F32, name="y", bufs=5)
             c = slice(BANK * h, BANK * (h + 1))
-            nc.scalar.activation(out=ep[:, c], in_=qps[h][:], func=ACT.Exp)
-            nc.scalar.activation(out=em[:, c], in_=qps[h][:], func=ACT.Exp, scale=-1.0)
+            nc.vector.scalar_tensor_tensor(out=y1_[j][:, c], in0=mps[j, h][:], scalar=sig[b][:, k:k + 1], in1=cq[:, c], op0=ALU.mult, op1=ALU.mult)
 
-        bcast_gain(0)
-        widen_v(0)
-        widen_v(1)
-        bcast_q(0, 6)
-        flip_x(0)
-        bcast_gain(1)
-        bcast_gain(2)
-        evac_gain(0, "v")
-        evac_x(0, "v")
-        flip_x(1)
-        exp_q(0)
-        evac_gain(1, "s")
-        bcast_q(1, 7)
-        widen_v(2)
-        quant_x(0)
-        evac_gain(2, "s")
-        evac_x(1, "s")
-        exp_q(1)
-        flip_x(2)
-        nc.gpsimd.tensor_tensor(out=cq[:], in0=ep[:], in1=em[:], op=ALU.add)
-        nc.gpsimd.tensor_tensor(out=sq[:], in0=ep[:], in1=em[:], op=ALU.subtract)
-
-        for i in range(TILES):
-            mm1(i)
-            if i + 2 < TILES:
-                evac_x(i + 2, "s")
-            if i >= 2:
-                evac_v(i - 2)
-            if i + 3 < TILES:
-                if i == 0:
-                    widen_v(3)
-                flip_x(i + 3)
-            if i >= 1:
-                flip_v(i - 1)
-            if i + 1 < TILES:
-                quant_x(i + 1)
-            if i >= 3:
-                quant_v(i - 3)
-            if i + 4 < TILES:
-                widen_v(i + 4)
-            for h in range(GD):
-                gain_v(i, h)
-                square_s(i, h)
-            if i % BATCH == BATCH - 1:
-                row_factors(i // BATCH)
-
-        mps, sqp, y_, q_, a_, sg_ = {}, {}, {}, {}, {}, {}
-
-        def mm2(j):
-            for h in range(HM):
-                acc = bank((2 * j + h) % 4, [P, BANK], F32, "mps")
-                mps[j, h] = acc
-                for g in range(GD):
-                    nc.tensor.matmul_mx(out=acc[:], lhsT=vcodes[j][:, P * g:P * (g + 1)].bitcast(FP8X4), lhsT_scale=vscales[j][:, P * g:P * (g + 1)],
-                                        rhs=z_sb[:, g, 1024 * h:1024 * (h + 1)].bitcast(FP4X4), rhs_scale=z_sc[:, g, BANK * h:BANK * (h + 1)],
-                                        start=(g == 0), stop=(g == GD - 1))
-
-        def logit_arg(j):
+        def logit_sub(j, h):
             b, k = j // BATCH, j % BATCH
-            y1 = ring.tile([P, M], F32, name="y1", bufs=2)
-            y_[j] = ring.tile([P, M], F32, name="y")
-            for h in range(HM):
-                c = slice(BANK * h, BANK * (h + 1))
-                nc.vector.scalar_tensor_tensor(out=y1[:, c], in0=mps[j, h][:], scalar=tau[b][:, k:k + 1], in1=cq[:, c], op0=ALU.mult, op1=ALU.mult)
-            for h in range(HM):
-                c = slice(BANK * h, BANK * (h + 1))
-                nc.vector.tensor_tensor(out=y_[j][:, c], in0=y1[:, c], in1=sqp[h][:], op=ALU.subtract)
+            c = slice(BANK * h, BANK * (h + 1))
+            nc.vector.scalar_tensor_tensor(out=y_[j][:, c], in0=sq[:, c] if j < 1 else sqp[h][:], scalar=nh[b][:, k:k + 1], in1=y1_[j][:, c], op0=ALU.mult, op1=ALU.add)
 
-        def square_abs(j):
-            b, k = j // BATCH, j % BATCH
-            q_[j] = ring.tile([P, M], F32, name="qq")
-            a_[j] = ring.tile([P, M], F32, name="aa")
-            nc.scalar.activation(out=q_[j][:], in_=y_[j][:], func=ACT.Square, scale=hfac[b][:, k:k + 1])
-            nc.scalar.activation(out=a_[j][:], in_=y_[j][:], func=ACT.Abs, scale=hfac[b][:, k:k + 1])
+        def absolute(j):
+            a_[j] = wsum[j]
+            nc.scalar.activation(out=a_[j][:], in_=y_[j][:], func=ACT.Abs)
+
+        def squared(j):
+            q_[j] = ring.tile([P, M], F32, name="qq", bufs=4)
+            if j in GSQ:
+                nc.gpsimd.tensor_tensor(out=q_[j][:], in0=a_[j][:], in1=a_[j][:], op=ALU.mult)
+            else:
+                nc.scalar.activation(out=q_[j][:], in_=y_[j][:], func=ACT.Square)
 
         def root(j):
             nc.scalar.activation(out=q_[j][:], in_=q_[j][:], func=ACT.Sqrt, bias=1.0)
 
         def add_root(j):
-            nc.gpsimd.tensor_tensor(out=wsum[j][:], in0=a_[j][:], in1=q_[j][:], op=ALU.add)
+            (nc.vector if j in VADD else nc.gpsimd).tensor_tensor(out=wsum[j][:], in0=a_[j][:], in1=q_[j][:], op=ALU.add)
 
         def sign_half(j):
             sg_[j] = ring.tile([P, M], BF16, name="sg")
-            nc.vector.tensor_scalar(out=sg_[j][:], in0=y_[j][:], scalar1=0.0, scalar2=0.5, op0=ALU.is_ge, op1=ALU.subtract)
+            if j in SSIGN:
+                nc.scalar.activation(out=sg_[j][:], in_=y_[j][:], func=ACT.Sign)
+            elif j in C2:
+                nc.vector.tensor_scalar(out=sg_[j][:], in0=y_[j][:], scalar1=0.0, scalar2=0.5, op0=ALU.is_ge, op1=ALU.subtract)
+            else:
+                nc.vector.scalar_tensor_tensor(out=sg_[j][:], in0=y_[j][:], scalar=0.0, in1=zp[0][:], op0=ALU.is_ge, op1=ALU.mult)
 
         def sign_gain(j):
-            nc.vector.tensor_tensor(out=gsign[j][:], in0=sg_[j][:], in1=zp[:], op=ALU.mult)
+            nc.vector.tensor_tensor(out=gsign[j][:], in0=sg_[j][:], in1=zp[0 if j in C2 else 1][:], op=ALU.mult if j in SSIGN or j in C2 else ALU.subtract)
 
-        for h in range(HM):
-            sqp[h] = bank(6 + h, [P, BANK], F32, "sqp")
-            nc.tensor.matmul(sqp[h][:], onesf[:], sq[:, BANK * h:BANK * (h + 1)], start=True, stop=True)
-        mm2(0)
-        evac_v(TILES - 2)
-        flip_v(TILES - 1)
-        quant_v(TILES - 3)
-        logit_arg(0)
-        mm2(1)
-        square_abs(0)
-        evac_v(TILES - 1)
-        quant_v(TILES - 2)
-        zp = bank(5, [P, M], BF16, "zp")
-        for h in range(HM):
-            nc.tensor.matmul(zp[:, BANK * h:BANK * (h + 1)], ones8[:], row_z[:, BANK * h:BANK * (h + 1)], start=True, stop=True)
-        for j in range(TILES):
-            if j >= 1:
-                square_abs(j)
-            root(j)
-            add_root(j)
-            if j + 1 < TILES:
-                logit_arg(j + 1)
-            if j == 0:
-                quant_v(TILES - 1)
-            if j + 2 < TILES:
-                mm2(j + 2)
-            if j >= 1:
-                sign_gain(j - 1)
-            sign_half(j)
-        sign_gain(TILES - 1)
+        def log(j, k, parts):
+            c = slice(M // parts * k, M // parts * (k + 1))
+            nc.scalar.activation(out=wsum[j][:, c], in_=wsum[j][:, c], func=ACT.Ln)
 
-        for j in range(TILES):
-            e = ring.tile([P, M], F32, name="e")
-            o = ring.tile([P, M], F32, name="o", bufs=4)
-            parts = 2 if j == TILES - 1 else 1
-            for k in range(parts):
-                c = slice(M // parts * k, M // parts * (k + 1))
-                nc.scalar.activation(out=e[:, c], in_=wsum[j][:, c], func=ACT.Ln)
-                nc.vector.tensor_tensor(out=o[:, c], in0=e[:, c], in1=gsign[j][:, c], op=ALU.mult)
-                nc.sync.dma_start(out=out[j * P:(j + 1) * P, c], in_=o[:, c])
+        def scaled(j, k, parts):
+            if k == 0:
+                o_[j] = ring.tile([P, M], F32, name="o", bufs=4)
+            c = slice(M // parts * k, M // parts * (k + 1))
+            nc.vector.scalar_tensor_tensor(out=o_[j][:, c], in0=wsum[j][:, c], scalar=8.0, in1=gsign[j][:, c], op0=ALU.mult, op1=ALU.mult)
+            nc.sync.dma_start(out=out[j * P:(j + 1) * P, c], in_=o_[j][:, c])
+
+        o_ = {}
+
+        const_two()
+        zero_wsc()
+        load_scale()
+        load_x(0)
+        const_neg()
+        widen(0)
+        load_x(1)
+        identity()
+        flip_x(0)
+        load_wsc()
+        warm_up()
+        load_w(0)
+        load_q()
+        row_tile(0)
+        load_x(2)
+        load_w(1)
+        load_gain()
+        evac_x(0)
+        widen(1)
+        flip_x(1)
+        zero_zsc()
+        widen(2)
+        flip_x(2)
+        load_w(2)
+        quant_x(0)
+        mm1(0, 0)
+        evac_x(1)
+        evac_x(2)
+        load_x(3)
+        load_x(4)
+        mm1(0, 1)
+        quant_x(1)
+        widen(3)
+        gain_v(0, 0)
+        gain_v(0, 1)
+        mm1(0, 2)
+        gain_v(0, 2)
+        mm1(1, 0)
+        gain_v(1, 0)
+        square_s(0, 0)
+        mm1(1, 1)
+        square_s(0, 1)
+        mm1(1, 2)
+        square_s(0, 2)
+        flip_v(0, 0)
+        quant_x(2)
+        load_x(5)
+        load_x(6)
+        flip_x(3)
+        square_s(1, 0)
+        widen(5)
+        gain_v(1, 2)
+        load_x(7)
+        load_z(0)
+        evac_v(0, 0)
+        column_factors()
+        mm1(2, 0)
+        mm1(2, 1)
+        evac_x(3)
+        square_s(1, 2)
+        gain_v(1, 1)
+        square_s(1, 1)
+        widen(4)
+        gain_v(2, 0)
+        gain_v(2, 1)
+        quant_x(3)
+        park(5)
+        load_z(1)
+        load_z(2)
+        flip_x(4)
+        flip_v(0, 1)
+        widen(6)
+        flip_x(5)
+        evac_x(4)
+        flip_v(1, 0)
+        row_sum(0)
+        square_s(2, 0)
+        square_s(2, 1)
+        quant_x(4)
+        row_tile(1)
+        mm1(2, 2)
+        mm1(3, 0)
+        evac_x(5)
+        gain_v(2, 2)
+        evac_v(1, 0)
+        mm1(3, 2)
+        row_root(0)
+        evac_v(0, 1)
+        row_factors(0)
+        fetch(5)
+        square_s(2, 2)
+        gain_v(3, 0)
+        mm1(3, 1)
+        gain_v(3, 1)
+        flip_v(2, 1)
+        flip_v(2, 0)
+        load_zsc()
+        square_s(3, 0)
+        gain_v(3, 2)
+        widen(7)
+        flip_v(1, 1)
+        square_s(3, 1)
+        evac_v(2, 0)
+        flip_x(6)
+        mm1(4, 0)
+        evac_x(6)
+        quant_v(0, 0)
+        gain_v(4, 0)
+        evac_v(1, 1)
+        quant_x(5)
+        mm1(4, 1)
+        square_s(3, 2)
+        row_sum(1)
+        square_s(4, 0)
+        gain_v(4, 1)
+        mm1(4, 2)
+        quant_x(6)
+        gain_v(4, 2)
+        flip_v(3, 1)
+        quant_v(1, 0)
+        flip_x(7)
+        square_s(4, 1)
+        mm1(5, 0)
+        gain_v(5, 0)
+        mm1(5, 1)
+        mm1(5, 2)
+        flip_v(3, 0)
+        evac_v(2, 1)
+        evac_x(7)
+        flip_v(4, 0)
+        flip_v(4, 1)
+        quant_v(1, 1)
+        square_s(4, 2)
+        mm1(6, 0)
+        quant_v(0, 1)
+        gain_v(5, 1)
+        evac_v(3, 0)
+        gain_v(5, 2)
+        quant_x(7)
+        row_root(1)
+        square_s(5, 1)
+        row_tile(2)
+        square_s(5, 0)
+        gain_v(6, 0)
+        mm2(0, 0)
+        quant_v(2, 0)
+        mm1(6, 2)
+        quant_v(3, 0)
+        mm1(6, 1)
+        evac_v(4, 0)
+        evac_v(4, 1)
+        flip_v(5, 1)
+        square_s(5, 2)
+        quant_v(2, 1)
+        gain_v(6, 2)
+        flip_v(5, 0)
+        square_s(6, 0)
+        mm1(7, 0)
+        quant_v(4, 0)
+        park(4)
+        evac_v(3, 1)
+        evac_v(5, 0)
+        gain_v(6, 1)
+        mm1(7, 1)
+        square_s(6, 1)
+        evac_v(5, 1)
+        fetch(4)
+        gain_v(7, 0)
+        square_s(7, 0)
+        gain_v(7, 1)
+        mm2(0, 1)
+        square_s(6, 2)
+        mm1(7, 2)
+        logit_mul(0, 0)
+        quant_v(3, 1)
+        row_factors(1)
+        flip_v(6, 0)
+        spread_sq(0)
+        logit_sub(0, 0)
+        gain_v(7, 2)
+        evac_v(6, 0)
+        flip_v(7, 0)
+        square_s(7, 1)
+        quant_v(5, 0)
+        flip_v(6, 1)
+        square_s(7, 2)
+        quant_v(4, 1)
+        evac_v(7, 0)
+        evac_v(6, 1)
+        row_sum(2)
+        row_root(2)
+        row_sum(3)
+        logit_mul(0, 1)
+        mm2(1, 0)
+        logit_sub(0, 1)
+        mm2(1, 1)
+        mm2(2, 0)
+        quant_v(7, 0)
+        logit_mul(1, 0)
+        quant_v(6, 0)
+        logit_sub(1, 0)
+        squared(0)
+        quant_v(5, 1)
+        spread_sq(1)
+        root(0)
+        logit_mul(1, 1)
+        mm2(3, 0)
+        mm2(2, 1)
+        absolute(0)
+        logit_mul(2, 0)
+        row_root(3)
+        logit_sub(1, 1)
+        squared(1)
+        mm2(3, 1)
+        logit_sub(2, 0)
+        absolute(1)
+        mm2(4, 0)
+        logit_mul(3, 0)
+        flip_v(7, 1)
+        load_zeta()
+        row_factors(2)
+        logit_mul(2, 1)
+        mm2(4, 1)
+        add_root(0)
+        logit_sub(2, 1)
+        root(1)
+        evac_v(7, 1)
+        logit_sub(3, 0)
+        mm2(5, 0)
+        squared(2)
+        absolute(2)
+        logit_mul(3, 1)
+        logit_mul(4, 0)
+        logit_sub(3, 1)
+        root(2)
+        logit_sub(4, 0)
+        row_factors(3)
+        spread_zeta(1)
+        mm2(5, 1)
+        quant_v(6, 1)
+        quant_v(7, 1)
+        squared(3)
+        absolute(3)
+        logit_mul(5, 0)
+        spread_zeta(0)
+        add_root(1)
+        logit_mul(4, 1)
+        logit_sub(4, 1)
+        squared(4)
+        sign_half(0)
+        logit_mul(5, 1)
+        add_root(2)
+        sign_half(1)
+        mm2(6, 1)
+        logit_sub(5, 0)
+        root(3)
+        logit_sub(5, 1)
+        absolute(4)
+        squared(5)
+        sign_gain(0)
+        mm2(6, 0)
+        absolute(5)
+        logit_mul(6, 0)
+        logit_mul(6, 1)
+        sign_gain(1)
+        logit_sub(6, 0)
+        mm2(7, 1)
+        logit_sub(6, 1)
+        add_root(3)
+        mm2(7, 0)
+        logit_mul(7, 0)
+        sign_half(2)
+        logit_mul(7, 1)
+        logit_sub(7, 0)
+        logit_sub(7, 1)
+        sign_half(3)
+        sign_half(4)
+        root(4)
+        sign_gain(2)
+        root(5)
+        sign_gain(4)
+        sign_gain(3)
+        absolute(6)
+        add_root(4)
+        sign_half(5)
+        squared(6)
+        squared(7)
+        root(6)
+        absolute(7)
+        sign_half(6)
+        add_root(5)
+        sign_half(7)
+        root(7)
+        log(0, 0, 1)
+        sign_gain(5)
+        sign_gain(6)
+        log(1, 0, 1)
+        scaled(0, 0, 1)
+        log(2, 0, 1)
+        log(3, 0, 1)
+        log(4, 0, 1)
+        add_root(6)
+        scaled(1, 0, 1)
+        add_root(7)
+        scaled(2, 0, 1)
+        scaled(3, 0, 1)
+        log(7, 0, 4)
+        scaled(4, 0, 1)
+        log(5, 0, 1)
+        log(6, 0, 1)
+        scaled(5, 0, 1)
+        log(7, 1, 4)
+        log(7, 3, 4)
+        scaled(6, 0, 1)
+        sign_gain(7)
+        scaled(7, 0, 4)
+        scaled(7, 1, 4)
+        log(7, 2, 4)
+        scaled(7, 3, 4)
+        scaled(7, 2, 4)

from contextlib import ExitStack

import concourse.mybir as mybir
from concourse.masks import make_identity

N, E, D, M = 1024, 1024, 1536, 1024
FLOPS = 2 * N * E * D + 2 * N * D * M

F32 = mybir.dt.float32
BF16 = mybir.dt.bfloat16
I32 = mybir.dt.int32
U32 = mybir.dt.uint32
U8 = mybir.dt.uint8
FP8 = mybir.dt.float8_e4m3fn
FP8X4 = mybir.dt.float8_e4m3fn_x4
FP4X4 = mybir.dt.float4_e2m1fn_x4
ALU = mybir.AluOpType
ACT = mybir.ActivationFunctionType

P = 128
BANK = 512
TILES = N // P
GE = E // 512
GD = D // 512
HM = M // BANK
BATCH = 2
GSQ = ()
WS = (1,)
C2 = ()
VEV = ()
SSIGN = ()
VADD = ()
VEX = (0,)
LOG2E = 1.4426950408889634


def tile_rmssinhcoshasinhlogits_kernel(tc, x_bytes, x_scale, w_words, w_scales, gain, z_words, z_scales, q, zeta, out):
    nc = tc.nc
    with ExitStack() as ctx:
        keep = ctx.enter_context(tc.tile_pool(name="keep", bufs=1))
        ring = ctx.enter_context(tc.tile_pool(name="ring", bufs=3))
        psum = ctx.enter_context(tc.psum_pool(name="psum", bufs=1))
        ctx.enter_context(tc.manual_schedule())

        def bank(b, shape, dtype, name):
            return psum.tile(shape, dtype, name=name, tag="bank%d" % b)

        x_in = [keep.tile([P, E], U8, name="x_in%d" % i) for i in range(TILES)]
        xsc = keep.tile([P, TILES * 8], F32, name="xsc")
        w_sb = [keep.tile([P, GE, 1024], U8, name="w_sb%d" % h, align_bytes=64) for h in range(GD)]
        w_sc = keep.tile([P, GE, D], U8, name="w_sc", align_bytes=64)
        z_sb = keep.tile([P, GD, 2 * M], U8, name="z_sb", align_bytes=64)
        z_sc = keep.tile([P, GD, M], U8, name="z_sc", align_bytes=64)
        gain_t = keep.tile([P, D], BF16, name="gain_t")
        zeta_t = keep.tile([P, M], BF16, name="zeta_t")
        ident = keep.tile([P, P], F32, name="ident")
        onesf = keep.tile([P, P], F32, name="onesf")
        onesb = keep.tile([P, P], BF16, name="onesb")
        halfb = keep.tile([P, P], BF16, name="halfb")
        c_two = keep.tile([P, 8], F32, name="c_two")
        c_neg = keep.tile([P, 8], F32, name="c_neg")
        warm = keep.tile([P, 1], F32, name="warm")
        cqs = [keep.tile([P, 8], BF16 if k == 0 else F32, name="cqs%d" % k) for k in range(6)]
        cq = keep.tile([P, M], F32, name="cq")
        sq = keep.tile([P, M], F32, name="sq")
        vcodes = [keep.tile([P, GD * P], U32, name="vcodes%d" % i, align_bytes=64) for i in range(TILES)]
        vscales = [keep.tile([P, GD * P], U8, name="vscales%d" % i, align_bytes=64) for i in range(TILES)]
        ssq = [keep.tile([P, BATCH, GD], F32, name="ssq%d" % b) for b in range(TILES // BATCH)]
        nh = [keep.tile([P, BATCH], F32, name="nh%d" % b) for b in range(TILES // BATCH)]
        sig = [keep.tile([P, BATCH], F32, name="sig%d" % b) for b in range(TILES // BATCH)]
        wsum = [keep.tile([P, M], F32, name="wsum%d" % i) for i in range(TILES)]
        gsign = [keep.tile([P, M], BF16, name="gsign%d" % i) for i in range(TILES)]

        def load_scale():
            nc.scalar.dma_start(out=xsc[:], in_=x_scale.rearrange("i j -> (i j)").partition_broadcast(P))

        def zero_wsc():
            nc.vector.memset(w_sc[:].bitcast(I32), 0)

        def zero_zsc():
            nc.vector.memset(z_sc[:].bitcast(I32), 0)

        def const_two():
            nc.gpsimd.memset(c_two[:], 2.0)

        def const_neg():
            nc.gpsimd.memset(c_neg[:], -1.0)

        def warm_up():
            nc.scalar.activation(out=warm[:], in_=c_two[:, 0:1], func=ACT.Sqrt)

        def identity():
            make_identity(nc, ident[:])

        def row_tile(k):
            t, v = ((onesf, 1.0), (onesb, 1.0), (halfb, 0.5))[k]
            nc.vector.memset(t[:], 0.0)
            nc.vector.memset(t[0:1, :], v)

        def load_x(i):
            nc.sync.dma_start(out=x_in[i][:], in_=x_bytes[i * P:(i + 1) * P, :])

        def load_w(h):
            src = w_words.rearrange("g p n -> p g n")[:, :, 1024 * h:1024 * (h + 1)]
            nc.sync.dma_start(out=w_sb[h][:].bitcast(I32), in_=src.bitcast(I32))

        def load_wsc():
            for r in range(4):
                nc.sync.dma_start(out=w_sc[32 * r:32 * r + 4, :, :].bitcast(I32), in_=w_scales[:, 4 * r:4 * r + 4, :].rearrange("g r n -> r g n").bitcast(I32))

        def load_q():
            nc.sync.dma_start(out=cqs[0][:], in_=q.rearrange("(p j) -> p j", j=8))

        def load_gain():
            nc.sync.dma_start(out=gain_t[:], in_=gain.partition_broadcast(P))

        def load_zeta():
            nc.sync.dma_start(out=zeta_t[:], in_=zeta.partition_broadcast(P))

        def load_z(g):
            nc.sync.dma_start(out=z_sb[:, g, :].bitcast(I32), in_=z_words[g].bitcast(I32))

        def load_zsc():
            for r in range(4):
                nc.sync.dma_start(out=z_sc[32 * r:32 * r + 4, :, :].bitcast(I32), in_=z_scales[:, 4 * r:4 * r + 4, :].rearrange("g r n -> r g n").bitcast(I32))

        def column_factors():
            g = nc.gpsimd
            t = cqs
            g.tensor_scalar(out=t[1][:], in0=t[0][:], scalar1=LOG2E, scalar2=0.0, op0=ALU.mult, op1=ALU.add)
            g.tensor_tensor(out=t[2][:], in0=c_two[:], in1=t[1][:], op=ALU.pow)
            g.tensor_tensor(out=t[3][:], in0=t[2][:], in1=c_neg[:], op=ALU.pow)
            g.tensor_tensor(out=t[4][:], in0=t[2][:], in1=t[3][:], op=ALU.add)
            g.tensor_tensor(out=t[5][:], in0=t[2][:], in1=t[3][:], op=ALU.subtract)

        def park(k):
            row = out[N - 8 + k:N - 7 + k, :]
            nc.sync.dma_start(out=row.rearrange("o (p j) -> (o p) j", j=8), in_=cqs[k][:])

        def fetch(k):
            row = out[N - 8 + k:N - 7 + k, :]
            nc.sync.dma_start(out=(cq if k == 4 else sq)[:], in_=row.rearrange("o c -> (o c)").partition_broadcast(P))

        xb, xps, xg, xcodes, xscales = {}, {}, {}, {}, {}
        vps, vg, vtps, vt = {}, {}, {}, {}
        XB = (4, 5, 6, 7, 4, 7, 6, 5)
        VB = ((5, 6), (4, 5), (7, 4), (6, 7), (4, 5), (4, 5), (4, 5), (4, 5))

        def widen(i):
            xb[i] = ring.tile([P, E], BF16, name="xb", align_bytes=64, bufs=4)
            for j in range(8):
                c = slice(P * j, P * (j + 1))
                if i in WS:
                    nc.scalar.activation(out=xb[i][:, c], in_=x_in[i][:, c].bitcast(FP8), func=ACT.Copy, scale=xsc[:, 8 * i + j:8 * i + j + 1])
                else:
                    nc.vector.tensor_scalar(out=xb[i][:, c], in0=x_in[i][:, c].bitcast(FP8), scalar1=xsc[:, 8 * i + j:8 * i + j + 1], scalar2=None, op0=ALU.mult)

        def flip_x(i):
            xps[i] = bank(XB[i], [P, GE, 2, P], F32, "xps")
            words = xb[i][:].bitcast(F32)
            for g in range(GE):
                for u in range(2):
                    nc.tensor.transpose(xps[i][:, g, u, :], words[:, 256 * g + u:256 * (g + 1):2], ident[:])

        def evac_x(i):
            xg[i] = ring.tile([P, GE, P, 4], BF16, name="xg", align_bytes=64)
            dst = xg[i][:].rearrange("p g n t -> p (g n t)").bitcast(F32).rearrange("p (g n u) -> p g n u", g=GE, u=2)
            src = xps[i][:].rearrange("p g u n -> p g n u")
            if i in VEX:
                nc.vector.tensor_copy(out=dst, in_=src)
            else:
                nc.scalar.copy(out=dst, in_=src)

        def quant_x(i):
            xcodes[i] = ring.tile([P, GE * P], U32, name="xcodes", align_bytes=64)
            xscales[i] = ring.tile([P, GE * P], U8, name="xscales", align_bytes=64)
            nc.vector.quantize_mx(out=xcodes[i][:].bitcast(FP8X4), scales=xscales[i][:], in_=xg[i][:].rearrange("p g n t -> p (g n t)"))

        def mm1(i, h):
            acc = bank((GD * i + h) % 4, [P, BANK], F32, "vps")
            vps[i, h] = acc
            for g in range(GE):
                nc.tensor.matmul_mx(out=acc[:], lhsT=xcodes[i][:, P * g:P * (g + 1)].bitcast(FP8X4), lhsT_scale=xscales[i][:, P * g:P * (g + 1)],
                                    rhs=w_sb[h][:, g, :].bitcast(FP4X4), rhs_scale=w_sc[:, g, BANK * h:BANK * (h + 1)], start=(g == 0), stop=(g == GE - 1))

        def gain_v(i, h):
            if h == 0:
                vg[i] = ring.tile([P, D], BF16, name="vg", align_bytes=64)
            c = slice(BANK * h, BANK * (h + 1))
            nc.vector.tensor_tensor(out=vg[i][:, c].rearrange("n (u p e) -> n u p e", u=2, e=2), in0=vps[i, h][:].rearrange("n (p u e) -> n u p e", u=2, e=2),
                                    in1=gain_t[:, c].rearrange("n (p u e) -> n u p e", u=2, e=2), op=ALU.mult)

        def square_s(i, h):
            junk = ring.tile([P, BANK], BF16, name="junk", bufs=2)
            nc.scalar.activation(out=junk[:], in_=vps[i, h][:], func=ACT.Square, accum_out=ssq[i // BATCH][:, i % BATCH, h:h + 1])

        def flip_v(i, k):
            words = vg[i][:].bitcast(F32)
            if k == 0:
                a = bank(VB[i][0], [P, 2, 2, P], F32, "vta")
                for g in range(2):
                    for u in range(2):
                        nc.tensor.transpose(a[:, g, u, :], words[:, 256 * g + P * u:256 * g + P * (u + 1)], ident[:])
            else:
                a = bank(VB[i][1], [P, 2, P], F32, "vtb")
                for u in range(2):
                    nc.tensor.transpose(a[:, u, :], words[:, 512 + P * u:512 + P * (u + 1)], ident[:])
            vtps[i, k] = a

        def evac_v(i, k):
            if k == 0:
                vt[i] = ring.tile([P, GD * P * 4], BF16, name="vt", align_bytes=64)
            words = vt[i][:].bitcast(F32)
            if k == 0:
                dst = words[:, 0:512].rearrange("p (g n u) -> p g n u", g=2, u=2)
                src = vtps[i, k][:].rearrange("p g u n -> p g n u")
            else:
                dst = words[:, 512:768].rearrange("p (n u) -> p n u", u=2)
                src = vtps[i, k][:].rearrange("p u n -> p n u")
            if (i, k) in VEV:
                nc.vector.tensor_copy(out=dst, in_=src)
            else:
                nc.scalar.copy(out=dst, in_=src)

        def quant_v(i, k):
            c = slice(0, 256) if k == 0 else slice(256, 384)
            nc.vector.quantize_mx(out=vcodes[i][:, c].bitcast(FP8X4), scales=vscales[i][:, c], in_=vt[i][:, 4 * c.start:4 * c.stop])

        rf = {}

        def row_sum(b):
            t = [keep.tile([P, BATCH], F32, name="rf%d_%d" % (b, k)) for k in range(9)]
            rf[b] = t
            g = nc.gpsimd
            g.tensor_tensor(out=t[0][:], in0=ssq[b][:, :, 0], in1=ssq[b][:, :, 1], op=ALU.add)
            g.tensor_tensor(out=t[1][:], in0=t[0][:], in1=ssq[b][:, :, 2], op=ALU.add)
            g.tensor_scalar(out=t[2][:], in0=t[1][:], scalar1=16.0 / D, scalar2=16e-6, op0=ALU.mult, op1=ALU.add)

        def row_root(b):
            nc.scalar.activation(out=rf[b][3][:], in_=rf[b][2][:], func=ACT.Sqrt)

        def row_factors(b):
            t = rf[b]
            g = nc.gpsimd
            two, neg = c_two[:, 0:BATCH], c_neg[:, 0:BATCH]
            g.tensor_scalar(out=t[4][:], in0=t[3][:], scalar1=LOG2E / 4, scalar2=0.0, op0=ALU.mult, op1=ALU.add)
            g.tensor_tensor(out=t[5][:], in0=two, in1=t[4][:], op=ALU.pow)
            g.tensor_tensor(out=t[6][:], in0=t[5][:], in1=neg, op=ALU.pow)
            g.tensor_tensor(out=t[7][:], in0=t[3][:], in1=neg, op=ALU.pow)
            g.tensor_tensor(out=t[8][:], in0=t[5][:], in1=t[6][:], op=ALU.subtract)
            g.tensor_tensor(out=sig[b][:], in0=t[8][:], in1=t[7][:], op=ALU.mult)
            g.tensor_tensor(out=t[0][:], in0=t[5][:], in1=t[6][:], op=ALU.add)
            g.tensor_scalar(out=nh[b][:], in0=t[0][:], scalar1=-0.25, scalar2=0.0, op0=ALU.mult, op1=ALU.add)

        mps, sqp, y_, y1_, q_, a_, sg_ = {}, {}, {}, {}, {}, {}, {}

        def spread_sq(h):
            sqp[h] = bank(6 + h, [P, BANK], F32, "sqp")
            nc.tensor.matmul(sqp[h][:], onesf[:], sq[:, BANK * h:BANK * (h + 1)], start=True, stop=True)

        def spread_zeta(k):
            zp[k] = bank(5 - k, [P, M], BF16, "zp%d" % k)
            for h in range(HM):
                c = slice(BANK * h, BANK * (h + 1))
                nc.tensor.matmul(zp[k][:, c], (halfb if k else onesb)[:], zeta_t[:, c], start=True, stop=True)

        zp = {}

        def mm2(j, h):
            acc = bank(6 + h if j == 0 else (2 * j + h) % 4, [P, BANK], F32, "mps")
            mps[j, h] = acc
            for g in range(GD):
                nc.tensor.matmul_mx(out=acc[:], lhsT=vcodes[j][:, P * g:P * (g + 1)].bitcast(FP8X4), lhsT_scale=vscales[j][:, P * g:P * (g + 1)],
                                    rhs=z_sb[:, g, 1024 * h:1024 * (h + 1)].bitcast(FP4X4), rhs_scale=z_sc[:, g, BANK * h:BANK * (h + 1)],
                                    start=(g == 0), stop=(g == GD - 1))

        def logit_mul(j, h):
            b, k = j // BATCH, j % BATCH
            if h == 0:
                y1_[j] = ring.tile([P, M], F32, name="y1", bufs=2)
                y_[j] = ring.tile([P, M], F32, name="y", bufs=5)
            c = slice(BANK * h, BANK * (h + 1))
            nc.vector.scalar_tensor_tensor(out=y1_[j][:, c], in0=mps[j, h][:], scalar=sig[b][:, k:k + 1], in1=cq[:, c], op0=ALU.mult, op1=ALU.mult)

        def logit_sub(j, h):
            b, k = j // BATCH, j % BATCH
            c = slice(BANK * h, BANK * (h + 1))
            nc.vector.scalar_tensor_tensor(out=y_[j][:, c], in0=sq[:, c] if j < 1 else sqp[h][:], scalar=nh[b][:, k:k + 1], in1=y1_[j][:, c], op0=ALU.mult, op1=ALU.add)

        def absolute(j):
            a_[j] = wsum[j]
            nc.scalar.activation(out=a_[j][:], in_=y_[j][:], func=ACT.Abs)

        def squared(j):
            q_[j] = ring.tile([P, M], F32, name="qq", bufs=4)
            if j in GSQ:
                nc.gpsimd.tensor_tensor(out=q_[j][:], in0=a_[j][:], in1=a_[j][:], op=ALU.mult)
            else:
                nc.scalar.activation(out=q_[j][:], in_=y_[j][:], func=ACT.Square)

        def root(j):
            nc.scalar.activation(out=q_[j][:], in_=q_[j][:], func=ACT.Sqrt, bias=1.0)

        def add_root(j):
            (nc.vector if j in VADD else nc.gpsimd).tensor_tensor(out=wsum[j][:], in0=a_[j][:], in1=q_[j][:], op=ALU.add)

        def sign_half(j):
            sg_[j] = ring.tile([P, M], BF16, name="sg")
            if j in SSIGN:
                nc.scalar.activation(out=sg_[j][:], in_=y_[j][:], func=ACT.Sign)
            elif j in C2:
                nc.vector.tensor_scalar(out=sg_[j][:], in0=y_[j][:], scalar1=0.0, scalar2=0.5, op0=ALU.is_ge, op1=ALU.subtract)
            else:
                nc.vector.scalar_tensor_tensor(out=sg_[j][:], in0=y_[j][:], scalar=0.0, in1=zp[0][:], op0=ALU.is_ge, op1=ALU.mult)

        def sign_gain(j):
            nc.vector.tensor_tensor(out=gsign[j][:], in0=sg_[j][:], in1=zp[0 if j in C2 else 1][:], op=ALU.mult if j in SSIGN or j in C2 else ALU.subtract)

        def log(j, k, parts):
            c = slice(M // parts * k, M // parts * (k + 1))
            nc.scalar.activation(out=wsum[j][:, c], in_=wsum[j][:, c], func=ACT.Ln)

        def scaled(j, k, parts):
            if k == 0:
                o_[j] = ring.tile([P, M], F32, name="o", bufs=4)
            c = slice(M // parts * k, M // parts * (k + 1))
            nc.vector.scalar_tensor_tensor(out=o_[j][:, c], in0=wsum[j][:, c], scalar=8.0, in1=gsign[j][:, c], op0=ALU.mult, op1=ALU.mult)
            nc.sync.dma_start(out=out[j * P:(j + 1) * P, c], in_=o_[j][:, c])

        o_ = {}

        const_two()
        zero_wsc()
        load_scale()
        load_x(0)
        const_neg()
        widen(0)
        load_x(1)
        identity()
        flip_x(0)
        load_wsc()
        warm_up()
        load_w(0)
        load_q()
        row_tile(0)
        load_x(2)
        load_w(1)
        load_gain()
        evac_x(0)
        widen(1)
        flip_x(1)
        zero_zsc()
        widen(2)
        flip_x(2)
        load_w(2)
        quant_x(0)
        mm1(0, 0)
        evac_x(1)
        evac_x(2)
        load_x(3)
        load_x(4)
        mm1(0, 1)
        quant_x(1)
        widen(3)
        gain_v(0, 0)
        gain_v(0, 1)
        mm1(0, 2)
        gain_v(0, 2)
        mm1(1, 0)
        gain_v(1, 0)
        square_s(0, 0)
        mm1(1, 1)
        square_s(0, 1)
        mm1(1, 2)
        square_s(0, 2)
        flip_v(0, 0)
        quant_x(2)
        load_x(5)
        load_x(6)
        flip_x(3)
        square_s(1, 0)
        widen(5)
        gain_v(1, 2)
        load_x(7)
        load_z(0)
        evac_v(0, 0)
        column_factors()
        mm1(2, 0)
        mm1(2, 1)
        evac_x(3)
        square_s(1, 2)
        gain_v(1, 1)
        square_s(1, 1)
        widen(4)
        gain_v(2, 0)
        gain_v(2, 1)
        quant_x(3)
        park(5)
        load_z(1)
        load_z(2)
        flip_x(4)
        flip_v(0, 1)
        widen(6)
        flip_x(5)
        evac_x(4)
        flip_v(1, 0)
        row_sum(0)
        square_s(2, 0)
        square_s(2, 1)
        quant_x(4)
        row_tile(1)
        mm1(2, 2)
        mm1(3, 0)
        evac_x(5)
        gain_v(2, 2)
        evac_v(1, 0)
        mm1(3, 2)
        row_root(0)
        evac_v(0, 1)
        row_factors(0)
        fetch(5)
        square_s(2, 2)
        gain_v(3, 0)
        mm1(3, 1)
        gain_v(3, 1)
        flip_v(2, 1)
        flip_v(2, 0)
        load_zsc()
        square_s(3, 0)
        gain_v(3, 2)
        widen(7)
        flip_v(1, 1)
        square_s(3, 1)
        evac_v(2, 0)
        flip_x(6)
        mm1(4, 0)
        evac_x(6)
        quant_v(0, 0)
        gain_v(4, 0)
        evac_v(1, 1)
        quant_x(5)
        mm1(4, 1)
        square_s(3, 2)
        row_sum(1)
        square_s(4, 0)
        gain_v(4, 1)
        mm1(4, 2)
        quant_x(6)
        gain_v(4, 2)
        flip_v(3, 1)
        quant_v(1, 0)
        flip_x(7)
        square_s(4, 1)
        mm1(5, 0)
        gain_v(5, 0)
        mm1(5, 1)
        mm1(5, 2)
        flip_v(3, 0)
        evac_v(2, 1)
        evac_x(7)
        flip_v(4, 0)
        flip_v(4, 1)
        quant_v(1, 1)
        square_s(4, 2)
        mm1(6, 0)
        quant_v(0, 1)
        gain_v(5, 1)
        evac_v(3, 0)
        gain_v(5, 2)
        quant_x(7)
        row_root(1)
        square_s(5, 1)
        row_tile(2)
        square_s(5, 0)
        gain_v(6, 0)
        mm2(0, 0)
        quant_v(2, 0)
        mm1(6, 2)
        quant_v(3, 0)
        mm1(6, 1)
        evac_v(4, 0)
        evac_v(4, 1)
        flip_v(5, 1)
        square_s(5, 2)
        quant_v(2, 1)
        gain_v(6, 2)
        flip_v(5, 0)
        square_s(6, 0)
        mm1(7, 0)
        quant_v(4, 0)
        park(4)
        evac_v(3, 1)
        evac_v(5, 0)
        gain_v(6, 1)
        mm1(7, 1)
        square_s(6, 1)
        evac_v(5, 1)
        fetch(4)
        gain_v(7, 0)
        square_s(7, 0)
        gain_v(7, 1)
        mm2(0, 1)
        square_s(6, 2)
        mm1(7, 2)
        logit_mul(0, 0)
        quant_v(3, 1)
        row_factors(1)
        flip_v(6, 0)
        spread_sq(0)
        logit_sub(0, 0)
        gain_v(7, 2)
        evac_v(6, 0)
        flip_v(7, 0)
        square_s(7, 1)
        quant_v(5, 0)
        flip_v(6, 1)
        square_s(7, 2)
        quant_v(4, 1)
        evac_v(7, 0)
        evac_v(6, 1)
        row_sum(2)
        row_root(2)
        row_sum(3)
        logit_mul(0, 1)
        mm2(1, 0)
        logit_sub(0, 1)
        mm2(1, 1)
        mm2(2, 0)
        quant_v(7, 0)
        logit_mul(1, 0)
        quant_v(6, 0)
        logit_sub(1, 0)
        squared(0)
        quant_v(5, 1)
        spread_sq(1)
        root(0)
        logit_mul(1, 1)
        mm2(3, 0)
        mm2(2, 1)
        absolute(0)
        logit_mul(2, 0)
        row_root(3)
        logit_sub(1, 1)
        squared(1)
        mm2(3, 1)
        logit_sub(2, 0)
        absolute(1)
        mm2(4, 0)
        logit_mul(3, 0)
        flip_v(7, 1)
        load_zeta()
        row_factors(2)
        logit_mul(2, 1)
        mm2(4, 1)
        add_root(0)
        logit_sub(2, 1)
        root(1)
        evac_v(7, 1)
        logit_sub(3, 0)
        mm2(5, 0)
        squared(2)
        absolute(2)
        logit_mul(3, 1)
        logit_mul(4, 0)
        logit_sub(3, 1)
        root(2)
        logit_sub(4, 0)
        row_factors(3)
        spread_zeta(1)
        mm2(5, 1)
        quant_v(6, 1)
        quant_v(7, 1)
        squared(3)
        absolute(3)
        logit_mul(5, 0)
        spread_zeta(0)
        add_root(1)
        logit_mul(4, 1)
        logit_sub(4, 1)
        squared(4)
        sign_half(0)
        logit_mul(5, 1)
        add_root(2)
        sign_half(1)
        mm2(6, 1)
        logit_sub(5, 0)
        root(3)
        logit_sub(5, 1)
        absolute(4)
        squared(5)
        sign_gain(0)
        mm2(6, 0)
        absolute(5)
        logit_mul(6, 0)
        logit_mul(6, 1)
        sign_gain(1)
        logit_sub(6, 0)
        mm2(7, 1)
        logit_sub(6, 1)
        add_root(3)
        mm2(7, 0)
        logit_mul(7, 0)
        sign_half(2)
        logit_mul(7, 1)
        logit_sub(7, 0)
        logit_sub(7, 1)
        sign_half(3)
        sign_half(4)
        root(4)
        sign_gain(2)
        root(5)
        sign_gain(4)
        sign_gain(3)
        absolute(6)
        add_root(4)
        sign_half(5)
        squared(6)
        squared(7)
        root(6)
        absolute(7)
        sign_half(6)
        add_root(5)
        sign_half(7)
        root(7)
        log(0, 0, 1)
        sign_gain(5)
        sign_gain(6)
        log(1, 0, 1)
        scaled(0, 0, 1)
        log(2, 0, 1)
        log(3, 0, 1)
        log(4, 0, 1)
        add_root(6)
        scaled(1, 0, 1)
        add_root(7)
        scaled(2, 0, 1)
        scaled(3, 0, 1)
        log(7, 0, 4)
        scaled(4, 0, 1)
        log(5, 0, 1)
        log(6, 0, 1)
        scaled(5, 0, 1)
        log(7, 1, 4)
        log(7, 3, 4)
        scaled(6, 0, 1)
        sign_gain(7)
        scaled(7, 0, 4)
        scaled(7, 1, 4)
        log(7, 2, 4)
        scaled(7, 3, 4)
        scaled(7, 2, 4)
